import numpy as np
import ml_dtypes


def mxq(x, axis, fmt="e4m3"):
    dtype, down = {"e4m3": (ml_dtypes.float8_e4m3fn, 7), "e5m2": (ml_dtypes.float8_e5m2, 14)}[fmt]
    v = np.moveaxis(np.asarray(x, np.float32).astype(ml_dtypes.bfloat16).astype(np.float64), axis, -1)
    blocks = v.reshape(v.shape[:-1] + (-1, 32))
    amax = np.abs(blocks).max(-1, keepdims=True)
    byte = np.maximum(np.where(amax > 0, np.frexp(amax)[1] - 1 + 127, 0) - down, 1)
    scale = np.exp2(byte - 127.0)
    codes = (blocks / scale).astype(np.float32).astype(dtype).astype(np.float64)
    return np.moveaxis((codes * scale).reshape(v.shape), -1, axis)


WIDE = False


def mx_kscale(k):
    if not WIDE:
        return np.ones(k)
    levels = np.array([30, -30])
    if k % 512:
        return np.exp2(np.random.permutation(np.resize(levels, k // 32))).repeat(32)
    a = np.empty((k // 512, 16))
    for p in range(k // 512):
        a[p, :8] = np.random.permutation(np.resize(levels, 8))
        for g in range(8):
            far = levels[np.abs(levels - a[p, g]) >= 10]
            a[p, g + 8] = far[np.random.randint(len(far))]
    return np.exp2(a.ravel()).repeat(32)


def f64(x):
    return np.asarray(x).astype(np.float64)


def striped(idx):
    return np.tile(np.asarray(idx).reshape(-1, 16).T, (8, 1)).astype(np.uint16)


def unstriped(offs):
    return offs[:16].T.reshape(-1).astype(np.int64)


E2M1 = np.array([0.0, 0.5, 1.0, 1.5, 2.0, 3.0, 4.0, 6.0, -0.0, -0.5, -1.0, -1.5, -2.0, -3.0, -4.0, -6.0])


def pack_weight(w, fmt):
    k, n = w.shape
    w = f64(np.asarray(w, np.float32).astype(ml_dtypes.bfloat16)).reshape(k // 32, 32, n)
    amax = np.abs(w).max(1)
    if fmt in ("e4m3", "e5m2"):
        byte = np.frexp(amax)[1] - 1 + 127 - (7 if fmt == "e4m3" else 14)
    else:
        mant, ex = np.frexp(amax / 6.0)
        byte = np.where(mant > 0.5, ex, ex - 1) + 127
    byte = np.clip(np.where(amax > 0, byte, 1), 1, 254)
    scaled = (w * np.exp2(127.0 - byte)[:, None, :]).reshape(k, n).astype(np.float32)
    by_word = np.ascontiguousarray(scaled.reshape(k // 512, 128, 4, n).transpose(0, 1, 3, 2))
    if fmt in ("e4m3", "e5m2"):
        words = by_word.astype(ml_dtypes.float8_e4m3fn if fmt == "e4m3" else ml_dtypes.float8_e5m2).view(np.uint8)
    else:
        c = by_word.astype(ml_dtypes.float4_e2m1fn).view(np.uint8) & 0xF
        words = (c[..., 0::2] | (c[..., 1::2] << 4)).reshape(k // 512, 128, 2 * n)
    return np.ascontiguousarray(words), np.ascontiguousarray(byte.astype(np.uint8).reshape(k // 512, 16, n))


def unpack_weight(words, scales, fmt):
    g, _, n = scales.shape
    words = np.ascontiguousarray(words).reshape(g, 128, n, -1)
    if fmt in ("e4m3", "e5m2"):
        vals = words.view(ml_dtypes.float8_e4m3fn if fmt == "e4m3" else ml_dtypes.float8_e5m2).astype(np.float64)
    else:
        nib = np.empty((g, 128, n, 4), np.uint8)
        nib[..., 0::2] = words & 0xF
        nib[..., 1::2] = words >> 4
        vals = E2M1[nib]
    vals = vals * np.repeat(np.exp2(scales.astype(np.float64) - 127.0), 8, axis=1)[..., None]
    return vals.transpose(0, 1, 3, 2).reshape(g * 512, n)


def bf(x):
    return np.asarray(x, np.float32).astype(ml_dtypes.bfloat16)


def planes(Y):
    r, m = Y.shape
    b = f64(bf(Y)).reshape(r // 32, 32, m)
    amax = np.abs(b).max(1)
    byte = np.clip(np.where(amax > 0, np.frexp(amax)[1] - 1 + 127 - 7, 1), 1, 254)
    codes = (b * np.exp2(127.0 - byte)[:, None, :]).reshape(r, m).astype(np.float32).astype(ml_dtypes.float8_e4m3fn).view(np.uint8)
    words = codes.reshape(r // 512, 128, 4, m).transpose(0, 1, 3, 2)
    return np.ascontiguousarray(words), np.ascontiguousarray(byte.astype(np.uint8).reshape(r // 512, 16, m))


K, T, J, R, N, Z = 1024, 1024, 384, 512, 512, 512


def setup_inputs():
    n = np.random.standard_normal
    idx = np.random.permutation(T)[:J]
    idx2 = np.random.permutation(T)[:J]
    idx3 = np.random.permutation(Z)[:J]
    fk = mx_kscale(K)
    fr = mx_kscale(R)
    wp = pack_weight(n((K, R)) * 1 / np.sqrt(K) * fk[:, None] * fr, "e5m2")
    wbp = pack_weight(n((R, N)) * 1 / np.sqrt(R) / fr[:, None], "e2m1")
    return {
        "xf": (n((K, T))).astype(np.float32),
        "fk": (np.random.uniform(0.5, 2.0, (K, 1)) / fk[:, None]).astype(np.float32),
        "w_words": wp[0],
        "w_scales": wp[1],
        "us": (np.random.uniform(0.5, 2.0, (R, 1)) * fr[:, None]).astype(np.float32),
        "wb_words": wbp[0],
        "wb_scales": wbp[1],
        "tz": (n((N, Z))).astype(np.float32),
        "offs": striped(idx),
        "offs2": striped(idx2),
        "offs3": striped(idx3),
    }


def reference(xf, fk, w_words, w_scales, us, wb_words, wb_scales, tz, offs, offs2, offs3):
    idx = unstriped(offs)
    idx2 = unstriped(offs2)
    idx3 = unstriped(offs3)
    wu = unpack_weight(w_words, w_scales, "e5m2")
    wbu = unpack_weight(wb_words, wb_scales, "e2m1")
    u = np.maximum(f64(xf)[:, idx], f64(xf)[:, idx2]) * f64(fk)
    uq = mxq(u, 0, "e4m3")
    a = wu.T @ uq
    pk1 = np.max(np.abs(a), axis=1, keepdims=True)
    hid = a / pk1 * f64(us)
    hidq = mxq(hid, 0, "e4m3")
    p = wbu.T @ hidq
    y = p * f64(tz)[:, idx3]
    words, scales = planes(y)
    return y, words, scales

@@ -1,0 +1,257 @@
+from contextlib import ExitStack
+
+import concourse.mybir as mybir
+
+K, T, J, R, N, Z = 1024, 1024, 384, 512, 512, 512
+FLOPS = 2 * K * R * J + 2 * R * N * J
+
+F32 = mybir.dt.float32
+BF16 = mybir.dt.bfloat16
+I32 = mybir.dt.int32
+U32 = mybir.dt.uint32
+U16 = mybir.dt.uint16
+U8 = mybir.dt.uint8
+E4M3 = mybir.dt.float8_e4m3fn_x4
+E5M2 = mybir.dt.float8_e5m2_x4
+E2M1 = mybir.dt.float4_e2m1fn_x4
+ALU = mybir.AluOpType
+COPY = mybir.ActivationFunctionType.Copy
+AX = mybir.AxisListType
+
+P = 128
+PACK = 4
+PASSES = K // (P * PACK)
+CH = 128
+CHUNKS = J // CH
+QUADS = 4
+VECTOR_GATHERS = (0, 1, 2, 3, 6, 7)
+
+
+def tile_list_largerpicks_peakscaled_timeslook_pl_kernel(
+    tc, xf, fk, w_words, w_scales, us, wb_words, wb_scales, tz, offs, offs2, offs3, out_0, out_1, out_2
+):
+    nc = tc.nc
+    with ExitStack() as ctx:
+        lists = ctx.enter_context(tc.tile_pool(name="lists", bufs=1))
+        sb = ctx.enter_context(tc.tile_pool(name="sb", bufs=1))
+        psum = ctx.enter_context(tc.psum_pool(name="psum", bufs=1))
+
+        l1 = lists.tile([P, J // 16], U16, name="l1")
+        l2 = lists.tile([P, J // 16], U16, name="l2")
+        l3 = lists.tile([P, J // 16], U16, name="l3")
+
+        x_sb = [sb.tile([P, T], F32, name=f"x{i}") for i in range(PASSES * PACK)]
+        tz_sb = [sb.tile([P, Z], F32, name=f"tz{t}") for t in range(PACK)]
+        fk_sb = sb.tile([P, PASSES, PACK], F32, name="fk_sb")
+        us_sb = sb.tile([P, PACK], F32, name="us_sb")
+        w_raw = sb.tile([P, PASSES, R], U32, name="w_raw")
+        wb_raw = sb.tile([P, N], U16, name="wb_raw")
+        sc_raw = sb.tile([P, (PASSES + 1) * R], U8, name="sc_raw")
+        w_deal = sb.tile([P, PASSES, R], U32, name="w_deal", align_bytes=64)
+        wb_deal = sb.tile([P, N], U16, name="wb_deal", align_bytes=64)
+        sc_deal = sb.tile([P, (PASSES + 1) * R], U8, name="sc_deal", align_bytes=64)
+
+        nc.vector.memset(sc_raw[:].bitcast(I32), 0)
+
+        x_rows = xf.rearrange("(a p t) c -> a t p c", p=P, t=PACK)
+        tz_rows = tz.rearrange("(p t) c -> t p c", t=PACK)
+
+        def load_x(i):
+            nc.sync.dma_start(out=x_sb[i][:], in_=x_rows[i // PACK, i % PACK])
+
+        def load_w_scales(q):
+            nc.sync.dma_start(
+                out=sc_raw[32 * q : 32 * q + 4, 0 : PASSES * R].bitcast(I32).rearrange("p (a c) -> p a c", a=PASSES),
+                in_=w_scales.bitcast(I32)[:, 4 * q : 4 * q + 4, :].rearrange("a r c -> r a c"),
+            )
+
+        def load_wb_scales(q):
+            nc.sync.dma_start(
+                out=sc_raw[32 * q : 32 * q + 4, PASSES * R :].bitcast(I32),
+                in_=wb_scales.bitcast(I32)[0, 4 * q : 4 * q + 4, :],
+            )
+
+        load_x(0)
+        nc.sync.dma_start(l1[:], offs)
+        nc.sync.dma_start(l2[:], offs2)
+        load_x(1)
+        load_w_scales(0)
+        load_w_scales(1)
+        load_x(2)
+        load_w_scales(2)
+        load_w_scales(3)
+        nc.sync.dma_start(
+            out=w_raw[:].bitcast(I32), in_=w_words.rearrange("a p n t -> p a (n t)").bitcast(I32)
+        )
+        load_wb_scales(0)
+        load_wb_scales(1)
+        load_x(3)
+        load_wb_scales(2)
+        load_wb_scales(3)
+        nc.sync.dma_start(out=fk_sb[:], in_=fk.rearrange("(a p t) o -> p a (t o)", p=P, t=PACK))
+        load_x(4)
+        load_x(5)
+        load_x(6)
+        nc.sync.dma_start(l3[:], offs3)
+        load_x(7)
+        nc.sync.dma_start(out=us_sb[:], in_=us.rearrange("(p t) o -> p (t o)", t=PACK))
+        nc.sync.dma_start(out=wb_raw[:].bitcast(I32), in_=wb_words[0].bitcast(I32))
+        for t in range(PACK):
+            nc.sync.dma_start(out=tz_sb[t][:], in_=tz_rows[t])
+
+        first = [sb.tile([P, PACK, J], F32, name=f"first{a}") for a in range(PASSES)]
+        second = [sb.tile([P, PACK, J], F32, name=f"second{a}") for a in range(PASSES)]
+        larger = [sb.tile([P, PACK, J], F32, name=f"larger{a}") for a in range(PASSES)]
+        u_bf = [sb.tile([P, J, PACK], BF16, name=f"u_bf{a}", align_bytes=64) for a in range(PASSES)]
+        u_codes = [sb.tile([P, J], U32, name=f"u_codes{a}", align_bytes=64) for a in range(PASSES)]
+        u_scales = [sb.tile([P, J], U8, name=f"u_scales{a}", align_bytes=64) for a in range(PASSES)]
+
+        def gather(on_vector, out, window, offsets):
+            if on_vector:
+                nc.vector.tensor_copy(out, window.indirect(offsets))
+            else:
+                nc.scalar.activation(out, window.indirect(offsets), COPY)
+
+        def pick(i):
+            a, t = divmod(i, PACK)
+            gather(False, first[a][:, t, :], x_sb[i][:], l1[:])
+            gather(i in VECTOR_GATHERS, second[a][:, t, :], x_sb[i][:], l2[:])
+            nc.vector.tensor_tensor(larger[a][:, t, :], first[a][:, t, :], second[a][:, t, :], ALU.max)
+
+        def scale_u(a, cols):
+            width = cols.stop - cols.start
+            nc.vector.tensor_tensor(
+                u_bf[a][:, cols, :].rearrange("p (c i) t -> p c t i", i=4),
+                larger[a][:, :, cols].rearrange("p t (c i) -> p c t i", i=4),
+                fk_sb[:, a, :].unsqueeze(1).unsqueeze(3).to_broadcast([P, width // 4, PACK, 4]),
+                ALU.mult,
+            )
+
+        def quantise(codes, scales, src, cols):
+            nc.vector.quantize_mx(
+                out=codes[:, cols].bitcast(E4M3),
+                scales=scales[:, cols],
+                in_=src[:, cols, :].rearrange("p j t -> p (j t)"),
+            )
+
+        chunk = [slice(c * CH, (c + 1) * CH) for c in range(CHUNKS)]
+        a_ps = [psum.tile([P, PACK, CH], F32, name=f"a_ps{c}") for c in range(CHUNKS)]
+        p_ps = [psum.tile([P, PACK, CH], F32, name=f"p_ps{c}") for c in range(CHUNKS)]
+
+        def first_product(a, c):
+            for t in range(PACK):
+                m = slice(t * P, (t + 1) * P)
+                nc.tensor.matmul_mx(
+                    out=a_ps[c][:, t, :],
+                    lhsT=w_deal[:, a, m].bitcast(E5M2),
+                    lhsT_scale=sc_deal[:, a * R + t * P : a * R + (t + 1) * P],
+                    rhs=u_codes[a][:, chunk[c]].bitcast(E4M3),
+                    rhs_scale=u_scales[a][:, chunk[c]],
+                    start=(a == 0 and t == 0),
+                    stop=(a == PASSES - 1 and t == PACK - 1),
+                )
+
+        for i in range(PACK - 1):
+            pick(i)
+        nc.scalar.copy(
+            w_deal[:].rearrange("p a (t m) -> p a m t", t=PACK),
+            w_raw[:].rearrange("p a (m t) -> p a m t", t=PACK),
+        )
+        pick(3)
+        scale_u(0, slice(0, J))
+        pick(4)
+        quantise(u_codes[0], u_scales[0], u_bf[0], slice(0, J))
+        pick(5)
+        nc.vector.tensor_copy(
+            sc_deal[:].rearrange("p (a t m) -> p a m t", t=PACK, m=P),
+            sc_raw[:].rearrange("p (a m t) -> p a m t", t=PACK, m=P),
+        )
+        for c in range(CHUNKS):
+            first_product(0, c)
+        pick(6)
+        pick(7)
+
+        scratch = sb.tile([P, PACK, PACK * CH], F32, name="scratch")
+        a_first = sb.tile([P, PACK * CH], F32, name="a_first")
+        a_flat = [a_first[:], scratch[:, 2, :], scratch[:, 3, :]]
+        a_sb = [v.rearrange("p (t j) -> p t j", t=PACK) for v in a_flat]
+        peaks = sb.tile([P, CHUNKS, PACK], F32, name="peaks")
+        peak = sb.tile([P, PACK], F32, name="peak")
+        inv = sb.tile([P, PACK], F32, name="inv")
+        factor = sb.tile([P, PACK], F32, name="factor")
+        tz_pick = scratch[:, :, 0:J]
+
+        scale_u(1, chunk[0])
+        for c in range(CHUNKS):
+            if c + 1 < CHUNKS:
+                scale_u(1, chunk[c + 1])
+            quantise(u_codes[1], u_scales[1], u_bf[1], chunk[c])
+            first_product(1, c)
+        for c in range(CHUNKS):
+            nc.scalar.activation(a_sb[c], a_ps[c][:], COPY)
+            nc.vector.tensor_reduce(peaks[:, c, :], a_sb[c], AX.X, ALU.max, apply_absolute_value=True)
+        nc.vector.tensor_reduce(peak[:], peaks[:].rearrange("p c t -> p t c"), AX.X, ALU.max)
+        nc.vector.reciprocal(inv[:], peak[:])
+        nc.vector.tensor_tensor(factor[:], inv[:], us_sb[:], ALU.mult)
+
+        nc.scalar.copy(
+            wb_deal[:].rearrange("p (t m) -> p m t", t=PACK),
+            wb_raw[:].rearrange("p (m t) -> p m t", t=PACK),
+        )
+        for t in range(PACK):
+            gather(False, tz_pick[:, t, :], tz_sb[t][:], l3[:])
+
+        h_bf = sb.tile([P, J, PACK], BF16, name="h_bf", align_bytes=64)
+        h_codes = sb.tile([P, J], U32, name="h_codes", align_bytes=64)
+        h_scales = sb.tile([P, J], U8, name="h_scales", align_bytes=64)
+        y_sb = [sb.tile([P, PACK, CH], F32, name=f"y{c}") for c in range(CHUNKS)]
+        y_bf = sb.tile([P, J, PACK], BF16, name="y_bf", align_bytes=64)
+        y_codes = sb.tile([P, J], U32, name="y_codes", align_bytes=64)
+        y_scales = sb.tile([P, J], U8, name="y_scales", align_bytes=64)
+        out_rows = out_0.rearrange("(p t) j -> p t j", t=PACK)
+        out_words = out_1[0].rearrange("p j t -> p (j t)").bitcast(I32)
+        wb_bytes = wb_deal[:].bitcast(U8)
+
+        def scale_h(c):
+            nc.vector.tensor_tensor(
+                h_bf[:, chunk[c], :],
+                a_ps[c][:].rearrange("p t j -> p j t"),
+                factor[:].unsqueeze(1).to_broadcast([P, CH, PACK]),
+                ALU.mult,
+            )
+
+        def second_product(c):
+            for t in range(PACK):
+                nc.tensor.matmul_mx(
+                    out=p_ps[c][:, t, :],
+                    lhsT=wb_bytes[:, 2 * t * P : 2 * (t + 1) * P].bitcast(E2M1),
+                    lhsT_scale=sc_deal[:, PASSES * R + t * P : PASSES * R + (t + 1) * P],
+                    rhs=h_codes[:, chunk[c]].bitcast(E4M3),
+                    rhs_scale=h_scales[:, chunk[c]],
+                    start=True,
+                    stop=True,
+                )
+
+        scale_h(0)
+        for c in range(CHUNKS):
+            if c + 1 < CHUNKS:
+                scale_h(c + 1)
+            quantise(h_codes, h_scales, h_bf, chunk[c])
+            second_product(c)
+
+        for c in range(CHUNKS):
+            nc.vector.tensor_tensor(y_sb[c][:], p_ps[c][:], tz_pick[:, :, chunk[c]], ALU.mult)
+            nc.sync.dma_start(out=out_rows[:, :, chunk[c]], in_=y_sb[c][:])
+            nc.scalar.copy(
+                y_bf[:, chunk[c], :].rearrange("p (c i) t -> p c t i", i=4),
+                y_sb[c][:].rearrange("p t (c i) -> p c t i", i=4),
+            )
+        for c in range(CHUNKS):
+            quantise(y_codes, y_scales, y_bf, chunk[c])
+            nc.sync.dma_start(out=out_words[:, chunk[c]], in_=y_codes[:, chunk[c]].bitcast(I32))
+        for q in range(QUADS):
+            queue = nc.sync if q % 2 == 0 else nc.scalar
+            queue.dma_start(
+                out=out_2.bitcast(I32)[0, 4 * q : 4 * q + 4, :],
+                in_=y_scales[32 * q : 32 * q + 4, :].bitcast(I32),
+            )

@@ -16,6 +16,7 @@ E5M2 = mybir.dt.float8_e5m2_x4
 E2M1 = mybir.dt.float4_e2m1fn_x4
 ALU = mybir.AluOpType
 COPY = mybir.ActivationFunctionType.Copy
+ABS = mybir.ActivationFunctionType.Abs
 AX = mybir.AxisListType
 
 P = 128
@@ -24,7 +25,7 @@ PASSES = K // (P * PACK)
 CH = 128
 CHUNKS = J // CH
 QUADS = 4
-VECTOR_GATHERS = (0, 1, 2, 3, 6, 7)
+VECTOR_GATHERS = (0, 1, 2, 3, 5)
 
 
 def tile_list_largerpicks_peakscaled_timeslook_pl_kernel(
@@ -40,8 +41,8 @@ def tile_list_largerpicks_peakscaled_timeslook_pl_kernel(
         l2 = lists.tile([P, J // 16], U16, name="l2")
         l3 = lists.tile([P, J // 16], U16, name="l3")
 
-        x_sb = [sb.tile([P, T], F32, name=f"x{i}") for i in range(PASSES * PACK)]
-        tz_sb = [sb.tile([P, Z], F32, name=f"tz{t}") for t in range(PACK)]
+        x_sb = [sb.tile([P, T], F32, name=f"x{i}") for i in range(PASSES * PACK - 2)]
+        x_last = sb.tile([P, 2, T], F32, name="x_last", tag="late")
         fk_sb = sb.tile([P, PASSES, PACK], F32, name="fk_sb")
         us_sb = sb.tile([P, PACK], F32, name="us_sb")
         w_raw = sb.tile([P, PASSES, R], U32, name="w_raw")
@@ -91,13 +92,12 @@ def tile_list_largerpicks_peakscaled_timeslook_pl_kernel(
         nc.sync.dma_start(out=fk_sb[:], in_=fk.rearrange("(a p t) o -> p a (t o)", p=P, t=PACK))
         load_x(4)
         load_x(5)
-        load_x(6)
+        nc.sync.dma_start(
+            out=x_last[:], in_=xf.rearrange("(a p t) c -> a p t c", p=P, t=PACK)[PASSES - 1, :, PACK - 2 :, :]
+        )
         nc.sync.dma_start(l3[:], offs3)
-        load_x(7)
         nc.sync.dma_start(out=us_sb[:], in_=us.rearrange("(p t) o -> p (t o)", t=PACK))
         nc.sync.dma_start(out=wb_raw[:].bitcast(I32), in_=wb_words[0].bitcast(I32))
-        for t in range(PACK):
-            nc.sync.dma_start(out=tz_sb[t][:], in_=tz_rows[t])
 
         first = [sb.tile([P, PACK, J], F32, name=f"first{a}") for a in range(PASSES)]
         second = [sb.tile([P, PACK, J], F32, name=f"second{a}") for a in range(PASSES)]
@@ -116,7 +116,9 @@ def tile_list_largerpicks_peakscaled_timeslook_pl_kernel(
             a, t = divmod(i, PACK)
             gather(False, first[a][:, t, :], x_sb[i][:], l1[:])
             gather(i in VECTOR_GATHERS, second[a][:, t, :], x_sb[i][:], l2[:])
-            nc.vector.tensor_tensor(larger[a][:, t, :], first[a][:, t, :], second[a][:, t, :], ALU.max)
+
+        def keep_larger(a, ts, cols):
+            nc.vector.tensor_tensor(larger[a][:, ts, cols], first[a][:, ts, cols], second[a][:, ts, cols], ALU.max)
 
         def scale_u(a, cols):
             width = cols.stop - cols.start
@@ -151,55 +153,73 @@ def tile_list_largerpicks_peakscaled_timeslook_pl_kernel(
                     stop=(a == PASSES - 1 and t == PACK - 1),
                 )
 
-        for i in range(PACK - 1):
-            pick(i)
+        every = slice(0, J)
+        low, high = slice(0, 2), slice(2, 4)
+        pick(0)
+        pick(1)
+        keep_larger(0, low, every)
+        pick(2)
         nc.scalar.copy(
             w_deal[:].rearrange("p a (t m) -> p a m t", t=PACK),
             w_raw[:].rearrange("p a (m t) -> p a m t", t=PACK),
         )
-        pick(3)
-        scale_u(0, slice(0, J))
-        pick(4)
-        quantise(u_codes[0], u_scales[0], u_bf[0], slice(0, J))
-        pick(5)
         nc.vector.tensor_copy(
-            sc_deal[:].rearrange("p (a t m) -> p a m t", t=PACK, m=P),
-            sc_raw[:].rearrange("p (a m t) -> p a m t", t=PACK, m=P),
+            sc_deal[:, 0 : PASSES * R].rearrange("p (a t m) -> p a m t", t=PACK, m=P),
+            sc_raw[:, 0 : PASSES * R].rearrange("p (a m t) -> p a m t", t=PACK, m=P),
         )
+        pick(3)
+        keep_larger(0, high, every)
+        scale_u(0, every)
+        nc.vector.tensor_copy(
+            sc_deal[:, PASSES * R :].rearrange("p (t m) -> p m t", t=PACK),
+            sc_raw[:, PASSES * R :].rearrange("p (m t) -> p m t", t=PACK),
+        )
+        quantise(u_codes[0], u_scales[0], u_bf[0], every)
+        pick(4)
+        pick(5)
+        keep_larger(1, low, every)
         for c in range(CHUNKS):
             first_product(0, c)
-        pick(6)
-        pick(7)
 
-        scratch = sb.tile([P, PACK, PACK * CH], F32, name="scratch")
-        a_first = sb.tile([P, PACK * CH], F32, name="a_first")
-        a_flat = [a_first[:], scratch[:, 2, :], scratch[:, 3, :]]
-        a_sb = [v.rearrange("p (t j) -> p t j", t=PACK) for v in a_flat]
-        peaks = sb.tile([P, CHUNKS, PACK], F32, name="peaks")
+        scratch = sb.tile([P, PACK * J], F32, name="scratch")
+        a_abs = [
+            scratch[:, s0 : s0 + PACK * CH].rearrange("p (t j) -> p t j", t=PACK) for s0 in (PACK * CH, 0)
+        ]
+        a_last = sb.tile([P, PACK, CH + CHUNKS - 1], F32, name="a_last")
         peak = sb.tile([P, PACK], F32, name="peak")
         inv = sb.tile([P, PACK], F32, name="inv")
         factor = sb.tile([P, PACK], F32, name="factor")
-        tz_pick = scratch[:, :, 0:J]
+        tz_pick = scratch[:].rearrange("p (t j) -> p t j", t=PACK)
 
-        scale_u(1, chunk[0])
         for c in range(CHUNKS):
-            if c + 1 < CHUNKS:
-                scale_u(1, chunk[c + 1])
+            entries = slice(c * CH // 16, (c + 1) * CH // 16)
+            for t in (2, 3):
+                gather(False, first[1][:, t, chunk[c]], x_last[:, t - 2, :], l1[:, entries])
+                gather(False, second[1][:, t, chunk[c]], x_last[:, t - 2, :], l2[:, entries])
+            keep_larger(1, high, chunk[c])
+            scale_u(1, chunk[c])
             quantise(u_codes[1], u_scales[1], u_bf[1], chunk[c])
             first_product(1, c)
-        for c in range(CHUNKS):
-            nc.scalar.activation(a_sb[c], a_ps[c][:], COPY)
-            nc.vector.tensor_reduce(peaks[:, c, :], a_sb[c], AX.X, ALU.max, apply_absolute_value=True)
-        nc.vector.tensor_reduce(peak[:], peaks[:].rearrange("p c t -> p t c"), AX.X, ALU.max)
-        nc.vector.reciprocal(inv[:], peak[:])
-        nc.vector.tensor_tensor(factor[:], inv[:], us_sb[:], ALU.mult)
-
         nc.scalar.copy(
             wb_deal[:].rearrange("p (t m) -> p m t", t=PACK),
             wb_raw[:].rearrange("p (m t) -> p m t", t=PACK),
         )
+        for c in range(CHUNKS - 1):
+            nc.scalar.activation(a_abs[c], a_ps[c][:], ABS)
+            nc.vector.tensor_reduce(a_last[:, :, CH + c], a_abs[c], AX.X, ALU.max)
+        for ts in (low, high):
+            nc.scalar.activation(a_last[:, ts, 0:CH], a_ps[CHUNKS - 1][:, ts, :], ABS)
+            nc.vector.tensor_reduce(peak[:, ts], a_last[:, ts, :], AX.X, ALU.max)
+        nc.vector.reciprocal(inv[:], peak[:])
+        nc.vector.tensor_tensor(factor[:], inv[:], us_sb[:], ALU.mult)
+
+        tz_sb = sb.tile([P, PACK, Z], F32, name="tz_sb", tag="late")
         for t in range(PACK):
-            gather(False, tz_pick[:, t, :], tz_sb[t][:], l3[:])
+            nc.sync.dma_start(out=tz_sb[:, t, :], in_=tz_rows[t])
+        for t in range(PACK):
+            for half in range(2):
+                cols = slice(half * J // 2, (half + 1) * J // 2)
+                gather(False, tz_pick[:, t, cols], tz_sb[:, t, :], l3[:, half * J // 32 : (half + 1) * J // 32])
 
         h_bf = sb.tile([P, J, PACK], BF16, name="h_bf", align_bytes=64)
         h_codes = sb.tile([P, J], U32, name="h_codes", align_bytes=64)
@@ -239,16 +259,23 @@ def tile_list_largerpicks_peakscaled_timeslook_pl_kernel(
             quantise(h_codes, h_scales, h_bf, chunk[c])
             second_product(c)
 
+        def round_y(copy, c, j0, j1):
+            copy(
+                y_bf[:, c * CH + j0 : c * CH + j1, :].rearrange("p (c i) t -> p c t i", i=4),
+                y_sb[c][:, :, j0:j1].rearrange("p t (c i) -> p c t i", i=4),
+            )
+
+        def store_words(cols):
+            quantise(y_codes, y_scales, y_bf, cols)
+            nc.sync.dma_start(out=out_words[:, cols], in_=y_codes[:, cols].bitcast(I32))
+
         for c in range(CHUNKS):
             nc.vector.tensor_tensor(y_sb[c][:], p_ps[c][:], tz_pick[:, :, chunk[c]], ALU.mult)
             nc.sync.dma_start(out=out_rows[:, :, chunk[c]], in_=y_sb[c][:])
-            nc.scalar.copy(
-                y_bf[:, chunk[c], :].rearrange("p (c i) t -> p c t i", i=4),
-                y_sb[c][:].rearrange("p t (c i) -> p c t i", i=4),
-            )
-        for c in range(CHUNKS):
-            quantise(y_codes, y_scales, y_bf, chunk[c])
-            nc.sync.dma_start(out=out_words[:, chunk[c]], in_=y_codes[:, chunk[c]].bitcast(I32))
+            round_y(nc.scalar.copy, c, 0, CH if c + 1 < CHUNKS else CH // 2)
+        store_words(slice(0, J - CH))
+        round_y(nc.vector.tensor_copy, CHUNKS - 1, CH // 2, CH)
+        store_words(chunk[CHUNKS - 1])
         for q in range(QUADS):
             queue = nc.sync if q % 2 == 0 else nc.scalar
             queue.dma_start(

@@ -25,7 +25,8 @@ PASSES = K // (P * PACK)
 CH = 128
 CHUNKS = J // CH
 QUADS = 4
-VECTOR_GATHERS = (0, 1, 2, 3, 5)
+VECTOR_FIRST = (1,)
+VECTOR_GATHERS = (0, 1, 3, 5, 6)
 
 
 def tile_list_largerpicks_peakscaled_timeslook_pl_kernel(
@@ -41,14 +42,14 @@ def tile_list_largerpicks_peakscaled_timeslook_pl_kernel(
         l2 = lists.tile([P, J // 16], U16, name="l2")
         l3 = lists.tile([P, J // 16], U16, name="l3")
 
-        x_sb = [sb.tile([P, T], F32, name=f"x{i}") for i in range(PASSES * PACK - 2)]
-        x_last = sb.tile([P, 2, T], F32, name="x_last", tag="late")
+        x_sb = [sb.tile([P, T], F32, name=f"x{i}") for i in range(PASSES * PACK)]
+        tz_sb = [sb.tile([P, Z], F32, name=f"tz{t}") for t in range(PACK)]
         fk_sb = sb.tile([P, PASSES, PACK], F32, name="fk_sb")
         us_sb = sb.tile([P, PACK], F32, name="us_sb")
-        w_raw = sb.tile([P, PASSES, R], U32, name="w_raw")
+        w_raw = [sb.tile([P, R], U32, name=f"w_raw{a}") for a in range(PASSES)]
         wb_raw = sb.tile([P, N], U16, name="wb_raw")
         sc_raw = sb.tile([P, (PASSES + 1) * R], U8, name="sc_raw")
-        w_deal = sb.tile([P, PASSES, R], U32, name="w_deal", align_bytes=64)
+        w_deal = [sb.tile([P, R], U32, name=f"w_deal{a}", align_bytes=64) for a in range(PASSES)]
         wb_deal = sb.tile([P, N], U16, name="wb_deal", align_bytes=64)
         sc_deal = sb.tile([P, (PASSES + 1) * R], U8, name="sc_deal", align_bytes=64)
 
@@ -72,32 +73,28 @@ def tile_list_largerpicks_peakscaled_timeslook_pl_kernel(
                 in_=wb_scales.bitcast(I32)[0, 4 * q : 4 * q + 4, :],
             )
 
+        def load_w(a):
+            nc.sync.dma_start(out=w_raw[a][:].bitcast(I32), in_=w_words[a].rearrange("p n t -> p (n t)").bitcast(I32))
+
         load_x(0)
         nc.sync.dma_start(l1[:], offs)
         nc.sync.dma_start(l2[:], offs2)
-        load_x(1)
-        load_w_scales(0)
-        load_w_scales(1)
-        load_x(2)
-        load_w_scales(2)
-        load_w_scales(3)
-        nc.sync.dma_start(
-            out=w_raw[:].bitcast(I32), in_=w_words.rearrange("a p n t -> p a (n t)").bitcast(I32)
-        )
-        load_wb_scales(0)
-        load_wb_scales(1)
-        load_x(3)
-        load_wb_scales(2)
-        load_wb_scales(3)
+        for i in range(1, PACK):
+            load_x(i)
+        for q in range(QUADS):
+            load_w_scales(q)
         nc.sync.dma_start(out=fk_sb[:], in_=fk.rearrange("(a p t) o -> p a (t o)", p=P, t=PACK))
-        load_x(4)
-        load_x(5)
-        nc.sync.dma_start(
-            out=x_last[:], in_=xf.rearrange("(a p t) c -> a p t c", p=P, t=PACK)[PASSES - 1, :, PACK - 2 :, :]
-        )
+        load_w(0)
+        for i in range(PACK, 2 * PACK):
+            load_x(i)
+        load_w(1)
+        nc.sync.dma_start(out=wb_raw[:].bitcast(I32), in_=wb_words[0].bitcast(I32))
         nc.sync.dma_start(l3[:], offs3)
         nc.sync.dma_start(out=us_sb[:], in_=us.rearrange("(p t) o -> p (t o)", t=PACK))
-        nc.sync.dma_start(out=wb_raw[:].bitcast(I32), in_=wb_words[0].bitcast(I32))
+        for t in range(PACK):
+            nc.sync.dma_start(out=tz_sb[t][:], in_=tz_rows[t])
+        for q in range(QUADS):
+            load_wb_scales(q)
 
         first = [sb.tile([P, PACK, J], F32, name=f"first{a}") for a in range(PASSES)]
         second = [sb.tile([P, PACK, J], F32, name=f"second{a}") for a in range(PASSES)]
@@ -114,7 +111,7 @@ def tile_list_largerpicks_peakscaled_timeslook_pl_kernel(
 
         def pick(i):
             a, t = divmod(i, PACK)
-            gather(False, first[a][:, t, :], x_sb[i][:], l1[:])
+            gather(i in VECTOR_FIRST, first[a][:, t, :], x_sb[i][:], l1[:])
             gather(i in VECTOR_GATHERS, second[a][:, t, :], x_sb[i][:], l2[:])
 
         def keep_larger(a, ts, cols):
@@ -145,7 +142,7 @@ def tile_list_largerpicks_peakscaled_timeslook_pl_kernel(
                 m = slice(t * P, (t + 1) * P)
                 nc.tensor.matmul_mx(
                     out=a_ps[c][:, t, :],
-                    lhsT=w_deal[:, a, m].bitcast(E5M2),
+                    lhsT=w_deal[a][:, m].bitcast(E5M2),
                     lhsT_scale=sc_deal[:, a * R + t * P : a * R + (t + 1) * P],
                     rhs=u_codes[a][:, chunk[c]].bitcast(E4M3),
                     rhs_scale=u_scales[a][:, chunk[c]],
@@ -153,39 +150,40 @@ def tile_list_largerpicks_peakscaled_timeslook_pl_kernel(
                     stop=(a == PASSES - 1 and t == PACK - 1),
                 )
 
+        def deal_w(a):
+            nc.scalar.copy(
+                w_deal[a][:].rearrange("p (t m) -> p m t", t=PACK),
+                w_raw[a][:].rearrange("p (m t) -> p m t", t=PACK),
+            )
+
         every = slice(0, J)
         low, high = slice(0, 2), slice(2, 4)
         pick(0)
         pick(1)
         keep_larger(0, low, every)
         pick(2)
-        nc.scalar.copy(
-            w_deal[:].rearrange("p a (t m) -> p a m t", t=PACK),
-            w_raw[:].rearrange("p a (m t) -> p a m t", t=PACK),
-        )
+        pick(3)
+        keep_larger(0, high, every)
+        deal_w(0)
+        scale_u(0, every)
         nc.vector.tensor_copy(
             sc_deal[:, 0 : PASSES * R].rearrange("p (a t m) -> p a m t", t=PACK, m=P),
             sc_raw[:, 0 : PASSES * R].rearrange("p (a m t) -> p a m t", t=PACK, m=P),
-        )
-        pick(3)
-        keep_larger(0, high, every)
-        scale_u(0, every)
-        nc.vector.tensor_copy(
-            sc_deal[:, PASSES * R :].rearrange("p (t m) -> p m t", t=PACK),
-            sc_raw[:, PASSES * R :].rearrange("p (m t) -> p m t", t=PACK),
         )
         quantise(u_codes[0], u_scales[0], u_bf[0], every)
         pick(4)
         pick(5)
         keep_larger(1, low, every)
+        pick(6)
+        keep_larger(1, slice(2, 3), every)
         for c in range(CHUNKS):
             first_product(0, c)
 
         scratch = sb.tile([P, PACK * J], F32, name="scratch")
-        a_abs = [
-            scratch[:, s0 : s0 + PACK * CH].rearrange("p (t j) -> p t j", t=PACK) for s0 in (PACK * CH, 0)
-        ]
-        a_last = sb.tile([P, PACK, CH + CHUNKS - 1], F32, name="a_last")
+        a_first = sb.tile([P, PACK, CH], F32, name="a_first")
+        a_abs = [a_first[:], scratch[:, 0 : PACK * CH].rearrange("p (t j) -> p t j", t=PACK)]
+        wide = CH + CHUNKS - 1
+        a_last = scratch[:, 2 * J : 2 * J + PACK * wide].rearrange("p (t j) -> p t j", t=PACK)
         peak = sb.tile([P, PACK], F32, name="peak")
         inv = sb.tile([P, PACK], F32, name="inv")
         factor = sb.tile([P, PACK], F32, name="factor")
@@ -193,10 +191,11 @@ def tile_list_largerpicks_peakscaled_timeslook_pl_kernel(
 
         for c in range(CHUNKS):
             entries = slice(c * CH // 16, (c + 1) * CH // 16)
-            for t in (2, 3):
-                gather(False, first[1][:, t, chunk[c]], x_last[:, t - 2, :], l1[:, entries])
-                gather(False, second[1][:, t, chunk[c]], x_last[:, t - 2, :], l2[:, entries])
-            keep_larger(1, high, chunk[c])
+            gather(False, first[1][:, 3, chunk[c]], x_sb[7][:], l1[:, entries])
+            gather(False, second[1][:, 3, chunk[c]], x_sb[7][:], l2[:, entries])
+        deal_w(1)
+        for c in range(CHUNKS):
+            keep_larger(1, slice(3, 4), chunk[c])
             scale_u(1, chunk[c])
             quantise(u_codes[1], u_scales[1], u_bf[1], chunk[c])
             first_product(1, c)
@@ -212,14 +211,13 @@ def tile_list_largerpicks_peakscaled_timeslook_pl_kernel(
             nc.vector.tensor_reduce(peak[:, ts], a_last[:, ts, :], AX.X, ALU.max)
         nc.vector.reciprocal(inv[:], peak[:])
         nc.vector.tensor_tensor(factor[:], inv[:], us_sb[:], ALU.mult)
+        nc.vector.tensor_copy(
+            sc_deal[:, PASSES * R :].rearrange("p (t m) -> p m t", t=PACK),
+            sc_raw[:, PASSES * R :].rearrange("p (m t) -> p m t", t=PACK),
+        )
 
-        tz_sb = sb.tile([P, PACK, Z], F32, name="tz_sb", tag="late")
         for t in range(PACK):
-            nc.sync.dma_start(out=tz_sb[:, t, :], in_=tz_rows[t])
-        for t in range(PACK):
-            for half in range(2):
-                cols = slice(half * J // 2, (half + 1) * J // 2)
-                gather(False, tz_pick[:, t, cols], tz_sb[:, t, :], l3[:, half * J // 32 : (half + 1) * J // 32])
+            gather(False, tz_pick[:, t, :], tz_sb[t][:], l3[:])
 
         h_bf = sb.tile([P, J, PACK], BF16, name="h_bf", align_bytes=64)
         h_codes = sb.tile([P, J], U32, name="h_codes", align_bytes=64)

@@ -25,8 +25,14 @@ PASSES = K // (P * PACK)
 CH = 128
 CHUNKS = J // CH
 QUADS = 4
+QUAD = P // QUADS
+SCALE_ROWS = 4
+ENTRIES = 16
+LINE = 4
+PAIR = 2
+LATE = PASSES * PACK - PAIR
 VECTOR_FIRST = (1,)
-VECTOR_GATHERS = (0, 1, 3, 5, 6)
+VECTOR_SECOND = (0, 1, 3)
 
 
 def tile_list_largerpicks_peakscaled_timeslook_pl_kernel(
@@ -38,63 +44,71 @@ def tile_list_largerpicks_peakscaled_timeslook_pl_kernel(
         sb = ctx.enter_context(tc.tile_pool(name="sb", bufs=1))
         psum = ctx.enter_context(tc.psum_pool(name="psum", bufs=1))
 
-        l1 = lists.tile([P, J // 16], U16, name="l1")
-        l2 = lists.tile([P, J // 16], U16, name="l2")
-        l3 = lists.tile([P, J // 16], U16, name="l3")
+        list1 = lists.tile([P, J // ENTRIES], U16, name="list1")
+        list2 = lists.tile([P, J // ENTRIES], U16, name="list2")
+        list3 = lists.tile([P, J // ENTRIES], U16, name="list3")
 
-        x_sb = [sb.tile([P, T], F32, name=f"x{i}") for i in range(PASSES * PACK)]
+        x_sb = [sb.tile([P, T], F32, name=f"x{i}") for i in range(LATE)]
+        x_late = sb.tile([P, PAIR, T], F32, name="x_late")
         tz_sb = [sb.tile([P, Z], F32, name=f"tz{t}") for t in range(PACK)]
         fk_sb = sb.tile([P, PASSES, PACK], F32, name="fk_sb")
         us_sb = sb.tile([P, PACK], F32, name="us_sb")
         w_raw = [sb.tile([P, R], U32, name=f"w_raw{a}") for a in range(PASSES)]
         wb_raw = sb.tile([P, N], U16, name="wb_raw")
-        sc_raw = sb.tile([P, (PASSES + 1) * R], U8, name="sc_raw")
+        wb_at = PASSES * R
+        sc_raw = sb.tile([P, wb_at + N], U8, name="sc_raw")
         w_deal = [sb.tile([P, R], U32, name=f"w_deal{a}", align_bytes=64) for a in range(PASSES)]
         wb_deal = sb.tile([P, N], U16, name="wb_deal", align_bytes=64)
-        sc_deal = sb.tile([P, (PASSES + 1) * R], U8, name="sc_deal", align_bytes=64)
+        sc_deal = sb.tile([P, wb_at + N], U8, name="sc_deal", align_bytes=64)
 
         nc.vector.memset(sc_raw[:].bitcast(I32), 0)
 
         x_rows = xf.rearrange("(a p t) c -> a t p c", p=P, t=PACK)
         tz_rows = tz.rearrange("(p t) c -> t p c", t=PACK)
 
+        def live(q):
+            return slice(QUAD * q, QUAD * q + SCALE_ROWS)
+
+        def blocks(q):
+            return slice(SCALE_ROWS * q, SCALE_ROWS * (q + 1))
+
         def load_x(i):
             nc.sync.dma_start(out=x_sb[i][:], in_=x_rows[i // PACK, i % PACK])
 
         def load_w_scales(q):
             nc.sync.dma_start(
-                out=sc_raw[32 * q : 32 * q + 4, 0 : PASSES * R].bitcast(I32).rearrange("p (a c) -> p a c", a=PASSES),
-                in_=w_scales.bitcast(I32)[:, 4 * q : 4 * q + 4, :].rearrange("a r c -> r a c"),
+                out=sc_raw[live(q), 0:wb_at].bitcast(I32).rearrange("p (a c) -> p a c", a=PASSES),
+                in_=w_scales.bitcast(I32)[:, blocks(q), :].rearrange("a r c -> r a c"),
             )
 
         def load_wb_scales(q):
-            nc.sync.dma_start(
-                out=sc_raw[32 * q : 32 * q + 4, PASSES * R :].bitcast(I32),
-                in_=wb_scales.bitcast(I32)[0, 4 * q : 4 * q + 4, :],
-            )
+            nc.sync.dma_start(out=sc_raw[live(q), wb_at:].bitcast(I32), in_=wb_scales.bitcast(I32)[0, blocks(q), :])
 
         def load_w(a):
             nc.sync.dma_start(out=w_raw[a][:].bitcast(I32), in_=w_words[a].rearrange("p n t -> p (n t)").bitcast(I32))
 
         load_x(0)
-        nc.sync.dma_start(l1[:], offs)
-        nc.sync.dma_start(l2[:], offs2)
+        nc.sync.dma_start(list1[:], offs)
+        nc.sync.dma_start(list2[:], offs2)
         for i in range(1, PACK):
             load_x(i)
         for q in range(QUADS):
             load_w_scales(q)
         nc.sync.dma_start(out=fk_sb[:], in_=fk.rearrange("(a p t) o -> p a (t o)", p=P, t=PACK))
         load_w(0)
-        for i in range(PACK, 2 * PACK):
-            load_x(i)
+        for t in range(PAIR):
+            load_x(PACK + t)
+            load_wb_scales(2 * t)
+            load_wb_scales(2 * t + 1)
+        nc.sync.dma_start(
+            out=x_late[:], in_=xf.rearrange("(a p t) c -> a p t c", p=P, t=PACK)[PASSES - 1, :, PACK - PAIR :, :]
+        )
         load_w(1)
         nc.sync.dma_start(out=wb_raw[:].bitcast(I32), in_=wb_words[0].bitcast(I32))
-        nc.sync.dma_start(l3[:], offs3)
+        nc.sync.dma_start(list3[:], offs3)
         nc.sync.dma_start(out=us_sb[:], in_=us.rearrange("(p t) o -> p (t o)", t=PACK))
         for t in range(PACK):
             nc.sync.dma_start(out=tz_sb[t][:], in_=tz_rows[t])
-        for q in range(QUADS):
-            load_wb_scales(q)
 
         first = [sb.tile([P, PACK, J], F32, name=f"first{a}") for a in range(PASSES)]
         second = [sb.tile([P, PACK, J], F32, name=f"second{a}") for a in range(PASSES)]
@@ -103,16 +117,18 @@ def tile_list_largerpicks_peakscaled_timeslook_pl_kernel(
         u_codes = [sb.tile([P, J], U32, name=f"u_codes{a}", align_bytes=64) for a in range(PASSES)]
         u_scales = [sb.tile([P, J], U8, name=f"u_scales{a}", align_bytes=64) for a in range(PASSES)]
 
-        def gather(on_vector, out, window, offsets):
-            if on_vector:
-                nc.vector.tensor_copy(out, window.indirect(offsets))
-            else:
-                nc.scalar.activation(out, window.indirect(offsets), COPY)
+        def gather_on_vector(out, window, offsets):
+            nc.vector.tensor_copy(out, window.indirect(offsets))
+
+        def gather_on_scalar(out, window, offsets):
+            nc.scalar.activation(out, window.indirect(offsets), COPY)
 
         def pick(i):
             a, t = divmod(i, PACK)
-            gather(i in VECTOR_FIRST, first[a][:, t, :], x_sb[i][:], l1[:])
-            gather(i in VECTOR_GATHERS, second[a][:, t, :], x_sb[i][:], l2[:])
+            by_first = gather_on_vector if i in VECTOR_FIRST else gather_on_scalar
+            by_second = gather_on_vector if i in VECTOR_SECOND else gather_on_scalar
+            by_first(first[a][:, t, :], x_sb[i][:], list1[:])
+            by_second(second[a][:, t, :], x_sb[i][:], list2[:])
 
         def keep_larger(a, ts, cols):
             nc.vector.tensor_tensor(larger[a][:, ts, cols], first[a][:, ts, cols], second[a][:, ts, cols], ALU.max)
@@ -120,9 +136,9 @@ def tile_list_largerpicks_peakscaled_timeslook_pl_kernel(
         def scale_u(a, cols):
             width = cols.stop - cols.start
             nc.vector.tensor_tensor(
-                u_bf[a][:, cols, :].rearrange("p (c i) t -> p c t i", i=4),
-                larger[a][:, :, cols].rearrange("p t (c i) -> p c t i", i=4),
-                fk_sb[:, a, :].unsqueeze(1).unsqueeze(3).to_broadcast([P, width // 4, PACK, 4]),
+                u_bf[a][:, cols, :].rearrange("p (c i) t -> p c t i", i=LINE),
+                larger[a][:, :, cols].rearrange("p t (c i) -> p c t i", i=LINE),
+                fk_sb[:, a, :].unsqueeze(1).unsqueeze(3).to_broadcast([P, width // LINE, PACK, LINE]),
                 ALU.mult,
             )
 
@@ -139,10 +155,9 @@ def tile_list_largerpicks_peakscaled_timeslook_pl_kernel(
 
         def first_product(a, c):
             for t in range(PACK):
-                m = slice(t * P, (t + 1) * P)
                 nc.tensor.matmul_mx(
                     out=a_ps[c][:, t, :],
-                    lhsT=w_deal[a][:, m].bitcast(E5M2),
+                    lhsT=w_deal[a][:, t * P : (t + 1) * P].bitcast(E5M2),
                     lhsT_scale=sc_deal[:, a * R + t * P : a * R + (t + 1) * P],
                     rhs=u_codes[a][:, chunk[c]].bitcast(E4M3),
                     rhs_scale=u_scales[a][:, chunk[c]],
@@ -150,74 +165,63 @@ def tile_list_largerpicks_peakscaled_timeslook_pl_kernel(
                     stop=(a == PASSES - 1 and t == PACK - 1),
                 )
 
-        def deal_w(a):
-            nc.scalar.copy(
-                w_deal[a][:].rearrange("p (t m) -> p m t", t=PACK),
-                w_raw[a][:].rearrange("p (m t) -> p m t", t=PACK),
-            )
+        def deal(copy, dealt, raw):
+            copy(dealt.rearrange("p (t m) -> p m t", t=PACK), raw.rearrange("p (m t) -> p m t", t=PACK))
 
         every = slice(0, J)
-        low, high = slice(0, 2), slice(2, 4)
-        pick(0)
-        pick(1)
-        keep_larger(0, low, every)
-        pick(2)
-        pick(3)
-        keep_larger(0, high, every)
-        deal_w(0)
+        low, high = slice(0, PAIR), slice(PAIR, PACK)
+        for ts in (low, high):
+            for t in range(ts.start, ts.stop):
+                pick(t)
+            keep_larger(0, ts, every)
+        deal(nc.vector.tensor_copy, w_deal[0][:], w_raw[0][:])
         scale_u(0, every)
         nc.vector.tensor_copy(
-            sc_deal[:, 0 : PASSES * R].rearrange("p (a t m) -> p a m t", t=PACK, m=P),
-            sc_raw[:, 0 : PASSES * R].rearrange("p (a m t) -> p a m t", t=PACK, m=P),
+            sc_deal[:, 0:wb_at].rearrange("p (a t m) -> p a m t", t=PACK, m=P),
+            sc_raw[:, 0:wb_at].rearrange("p (a m t) -> p a m t", t=PACK, m=P),
         )
         quantise(u_codes[0], u_scales[0], u_bf[0], every)
-        pick(4)
-        pick(5)
+        for t in range(PAIR):
+            pick(PACK + t)
+        deal(nc.vector.tensor_copy, sc_deal[:, wb_at:], sc_raw[:, wb_at:])
         keep_larger(1, low, every)
-        pick(6)
-        keep_larger(1, slice(2, 3), every)
         for c in range(CHUNKS):
             first_product(0, c)
 
-        scratch = sb.tile([P, PACK * J], F32, name="scratch")
+        shared = sb.tile([P, PACK * J], F32, name="shared")
         a_first = sb.tile([P, PACK, CH], F32, name="a_first")
-        a_abs = [a_first[:], scratch[:, 0 : PACK * CH].rearrange("p (t j) -> p t j", t=PACK)]
-        wide = CH + CHUNKS - 1
-        a_last = scratch[:, 2 * J : 2 * J + PACK * wide].rearrange("p (t j) -> p t j", t=PACK)
+        a_abs = [a_first[:], shared[:, 0 : PACK * CH].rearrange("p (t j) -> p t j", t=PACK)]
+        a_last = shared[:, PAIR * J : PAIR * J + PACK * CH].rearrange("p (t j) -> p t j", t=PACK)
+        peaks = sb.tile([P, CHUNKS, PACK], F32, name="peaks")
         peak = sb.tile([P, PACK], F32, name="peak")
         inv = sb.tile([P, PACK], F32, name="inv")
         factor = sb.tile([P, PACK], F32, name="factor")
-        tz_pick = scratch[:].rearrange("p (t j) -> p t j", t=PACK)
+        tz_pick = shared[:].rearrange("p (t j) -> p t j", t=PACK)
 
+        deal(nc.vector.tensor_copy, w_deal[1][:], w_raw[1][:])
         for c in range(CHUNKS):
-            entries = slice(c * CH // 16, (c + 1) * CH // 16)
-            gather(False, first[1][:, 3, chunk[c]], x_sb[7][:], l1[:, entries])
-            gather(False, second[1][:, 3, chunk[c]], x_sb[7][:], l2[:, entries])
-        deal_w(1)
-        for c in range(CHUNKS):
-            keep_larger(1, slice(3, 4), chunk[c])
+            entries = slice(c * CH // ENTRIES, (c + 1) * CH // ENTRIES)
+            for t in range(PAIR):
+                gather_on_scalar(first[1][:, PAIR + t, chunk[c]], x_late[:, t, :], list1[:, entries])
+                gather_on_scalar(second[1][:, PAIR + t, chunk[c]], x_late[:, t, :], list2[:, entries])
+            keep_larger(1, high, chunk[c])
             scale_u(1, chunk[c])
             quantise(u_codes[1], u_scales[1], u_bf[1], chunk[c])
             first_product(1, c)
-        nc.scalar.copy(
-            wb_deal[:].rearrange("p (t m) -> p m t", t=PACK),
-            wb_raw[:].rearrange("p (m t) -> p m t", t=PACK),
-        )
+        deal(nc.scalar.copy, wb_deal[:], wb_raw[:])
+
         for c in range(CHUNKS - 1):
             nc.scalar.activation(a_abs[c], a_ps[c][:], ABS)
-            nc.vector.tensor_reduce(a_last[:, :, CH + c], a_abs[c], AX.X, ALU.max)
+            nc.vector.tensor_reduce(peaks[:, c, :], a_abs[c], AX.X, ALU.max)
         for ts in (low, high):
-            nc.scalar.activation(a_last[:, ts, 0:CH], a_ps[CHUNKS - 1][:, ts, :], ABS)
-            nc.vector.tensor_reduce(peak[:, ts], a_last[:, ts, :], AX.X, ALU.max)
+            nc.scalar.activation(a_last[:, ts, :], a_ps[CHUNKS - 1][:, ts, :], ABS)
+            nc.vector.tensor_reduce(peaks[:, CHUNKS - 1, ts], a_last[:, ts, :], AX.X, ALU.max)
+        nc.vector.tensor_reduce(peak[:], peaks[:].rearrange("p c t -> p t c"), AX.X, ALU.max)
         nc.vector.reciprocal(inv[:], peak[:])
         nc.vector.tensor_tensor(factor[:], inv[:], us_sb[:], ALU.mult)
-        nc.vector.tensor_copy(
-            sc_deal[:, PASSES * R :].rearrange("p (t m) -> p m t", t=PACK),
-            sc_raw[:, PASSES * R :].rearrange("p (m t) -> p m t", t=PACK),
-        )
 
         for t in range(PACK):
-            gather(False, tz_pick[:, t, :], tz_sb[t][:], l3[:])
+            gather_on_scalar(tz_pick[:, t, :], tz_sb[t][:], list3[:])
 
         h_bf = sb.tile([P, J, PACK], BF16, name="h_bf", align_bytes=64)
         h_codes = sb.tile([P, J], U32, name="h_codes", align_bytes=64)
@@ -243,7 +247,7 @@ def tile_list_largerpicks_peakscaled_timeslook_pl_kernel(
                 nc.tensor.matmul_mx(
                     out=p_ps[c][:, t, :],
                     lhsT=wb_bytes[:, 2 * t * P : 2 * (t + 1) * P].bitcast(E2M1),
-                    lhsT_scale=sc_deal[:, PASSES * R + t * P : PASSES * R + (t + 1) * P],
+                    lhsT_scale=sc_deal[:, wb_at + t * P : wb_at + (t + 1) * P],
                     rhs=h_codes[:, chunk[c]].bitcast(E4M3),
                     rhs_scale=h_scales[:, chunk[c]],
                     start=True,
@@ -259,8 +263,8 @@ def tile_list_largerpicks_peakscaled_timeslook_pl_kernel(
 
         def round_y(copy, c, j0, j1):
             copy(
-                y_bf[:, c * CH + j0 : c * CH + j1, :].rearrange("p (c i) t -> p c t i", i=4),
-                y_sb[c][:, :, j0:j1].rearrange("p t (c i) -> p c t i", i=4),
+                y_bf[:, c * CH + j0 : c * CH + j1, :].rearrange("p (c i) t -> p c t i", i=LINE),
+                y_sb[c][:, :, j0:j1].rearrange("p t (c i) -> p c t i", i=LINE),
             )
 
         def store_words(cols):
@@ -276,7 +280,4 @@ def tile_list_largerpicks_peakscaled_timeslook_pl_kernel(
         store_words(chunk[CHUNKS - 1])
         for q in range(QUADS):
             queue = nc.sync if q % 2 == 0 else nc.scalar
-            queue.dma_start(
-                out=out_2.bitcast(I32)[0, 4 * q : 4 * q + 4, :],
-                in_=y_scales[32 * q : 32 * q + 4, :].bitcast(I32),
-            )
+            queue.dma_start(out=out_2.bitcast(I32)[0, blocks(q), :], in_=y_scales[live(q), :].bitcast(I32))

from contextlib import ExitStack

import concourse.mybir as mybir

K, T, J, R, N, Z = 1024, 1024, 384, 512, 512, 512
FLOPS = 2 * K * R * J + 2 * R * N * J

F32 = mybir.dt.float32
BF16 = mybir.dt.bfloat16
I32 = mybir.dt.int32
U32 = mybir.dt.uint32
U16 = mybir.dt.uint16
U8 = mybir.dt.uint8
E4M3 = mybir.dt.float8_e4m3fn_x4
E5M2 = mybir.dt.float8_e5m2_x4
E2M1 = mybir.dt.float4_e2m1fn_x4
ALU = mybir.AluOpType
COPY = mybir.ActivationFunctionType.Copy
ABS = mybir.ActivationFunctionType.Abs
AX = mybir.AxisListType

P = 128
PACK = 4
PASSES = K // (P * PACK)
CH = 128
CHUNKS = J // CH
QUADS = 4
QUAD = P // QUADS
SCALE_ROWS = 4
ENTRIES = 16
LINE = 4
PAIR = 2
LATE = PASSES * PACK - PAIR
VECTOR_FIRST = (1,)
VECTOR_SECOND = (0, 1, 3)


def tile_list_largerpicks_peakscaled_timeslook_pl_kernel(
    tc, xf, fk, w_words, w_scales, us, wb_words, wb_scales, tz, offs, offs2, offs3, out_0, out_1, out_2
):
    nc = tc.nc
    with ExitStack() as ctx:
        lists = ctx.enter_context(tc.tile_pool(name="lists", bufs=1))
        sb = ctx.enter_context(tc.tile_pool(name="sb", bufs=1))
        psum = ctx.enter_context(tc.psum_pool(name="psum", bufs=1))

        list1 = lists.tile([P, J // ENTRIES], U16, name="list1")
        list2 = lists.tile([P, J // ENTRIES], U16, name="list2")
        list3 = lists.tile([P, J // ENTRIES], U16, name="list3")

        x_sb = [sb.tile([P, T], F32, name=f"x{i}") for i in range(LATE)]
        x_late = sb.tile([P, PAIR, T], F32, name="x_late")
        tz_sb = [sb.tile([P, Z], F32, name=f"tz{t}") for t in range(PACK)]
        fk_sb = sb.tile([P, PASSES, PACK], F32, name="fk_sb")
        us_sb = sb.tile([P, PACK], F32, name="us_sb")
        w_raw = [sb.tile([P, R], U32, name=f"w_raw{a}") for a in range(PASSES)]
        wb_raw = sb.tile([P, N], U16, name="wb_raw")
        wb_at = PASSES * R
        sc_raw = sb.tile([P, wb_at + N], U8, name="sc_raw")
        w_deal = [sb.tile([P, R], U32, name=f"w_deal{a}", align_bytes=64) for a in range(PASSES)]
        wb_deal = sb.tile([P, N], U16, name="wb_deal", align_bytes=64)
        sc_deal = sb.tile([P, wb_at + N], U8, name="sc_deal", align_bytes=64)

        nc.vector.memset(sc_raw[:].bitcast(I32), 0)

        x_rows = xf.rearrange("(a p t) c -> a t p c", p=P, t=PACK)
        tz_rows = tz.rearrange("(p t) c -> t p c", t=PACK)

        def live(q):
            return slice(QUAD * q, QUAD * q + SCALE_ROWS)

        def blocks(q):
            return slice(SCALE_ROWS * q, SCALE_ROWS * (q + 1))

        def load_x(i):
            nc.sync.dma_start(out=x_sb[i][:], in_=x_rows[i // PACK, i % PACK])

        def load_w_scales(q):
            nc.sync.dma_start(
                out=sc_raw[live(q), 0:wb_at].bitcast(I32).rearrange("p (a c) -> p a c", a=PASSES),
                in_=w_scales.bitcast(I32)[:, blocks(q), :].rearrange("a r c -> r a c"),
            )

        def load_wb_scales(q):
            nc.sync.dma_start(out=sc_raw[live(q), wb_at:].bitcast(I32), in_=wb_scales.bitcast(I32)[0, blocks(q), :])

        def load_w(a):
            nc.sync.dma_start(out=w_raw[a][:].bitcast(I32), in_=w_words[a].rearrange("p n t -> p (n t)").bitcast(I32))

        load_x(0)
        nc.sync.dma_start(list1[:], offs)
        nc.sync.dma_start(list2[:], offs2)
        for i in range(1, PACK):
            load_x(i)
        for q in range(QUADS):
            load_w_scales(q)
        nc.sync.dma_start(out=fk_sb[:], in_=fk.rearrange("(a p t) o -> p a (t o)", p=P, t=PACK))
        load_w(0)
        for t in range(PAIR):
            load_x(PACK + t)
            load_wb_scales(2 * t)
            load_wb_scales(2 * t + 1)
        nc.sync.dma_start(
            out=x_late[:], in_=xf.rearrange("(a p t) c -> a p t c", p=P, t=PACK)[PASSES - 1, :, PACK - PAIR :, :]
        )
        load_w(1)
        nc.sync.dma_start(out=wb_raw[:].bitcast(I32), in_=wb_words[0].bitcast(I32))
        nc.sync.dma_start(list3[:], offs3)
        nc.sync.dma_start(out=us_sb[:], in_=us.rearrange("(p t) o -> p (t o)", t=PACK))
        for t in range(PACK):
            nc.sync.dma_start(out=tz_sb[t][:], in_=tz_rows[t])

        first = [sb.tile([P, PACK, J], F32, name=f"first{a}") for a in range(PASSES)]
        second = [sb.tile([P, PACK, J], F32, name=f"second{a}") for a in range(PASSES)]
        larger = [sb.tile([P, PACK, J], F32, name=f"larger{a}") for a in range(PASSES)]
        u_bf = [sb.tile([P, J, PACK], BF16, name=f"u_bf{a}", align_bytes=64) for a in range(PASSES)]
        u_codes = [sb.tile([P, J], U32, name=f"u_codes{a}", align_bytes=64) for a in range(PASSES)]
        u_scales = [sb.tile([P, J], U8, name=f"u_scales{a}", align_bytes=64) for a in range(PASSES)]

        def gather_on_vector(out, window, offsets):
            nc.vector.tensor_copy(out, window.indirect(offsets))

        def gather_on_scalar(out, window, offsets):
            nc.scalar.activation(out, window.indirect(offsets), COPY)

        def pick(i):
            a, t = divmod(i, PACK)
            by_first = gather_on_vector if i in VECTOR_FIRST else gather_on_scalar
            by_second = gather_on_vector if i in VECTOR_SECOND else gather_on_scalar
            by_first(first[a][:, t, :], x_sb[i][:], list1[:])
            by_second(second[a][:, t, :], x_sb[i][:], list2[:])

        def keep_larger(a, ts, cols):
            nc.vector.tensor_tensor(larger[a][:, ts, cols], first[a][:, ts, cols], second[a][:, ts, cols], ALU.max)

        def scale_u(a, cols):
            width = cols.stop - cols.start
            nc.vector.tensor_tensor(
                u_bf[a][:, cols, :].rearrange("p (c i) t -> p c t i", i=LINE),
                larger[a][:, :, cols].rearrange("p t (c i) -> p c t i", i=LINE),
                fk_sb[:, a, :].unsqueeze(1).unsqueeze(3).to_broadcast([P, width // LINE, PACK, LINE]),
                ALU.mult,
            )

        def quantise(codes, scales, src, cols):
            nc.vector.quantize_mx(
                out=codes[:, cols].bitcast(E4M3),
                scales=scales[:, cols],
                in_=src[:, cols, :].rearrange("p j t -> p (j t)"),
            )

        chunk = [slice(c * CH, (c + 1) * CH) for c in range(CHUNKS)]
        a_ps = [psum.tile([P, PACK, CH], F32, name=f"a_ps{c}") for c in range(CHUNKS)]
        p_ps = [psum.tile([P, PACK, CH], F32, name=f"p_ps{c}") for c in range(CHUNKS)]

        def first_product(a, c):
            for t in range(PACK):
                nc.tensor.matmul_mx(
                    out=a_ps[c][:, t, :],
                    lhsT=w_deal[a][:, t * P : (t + 1) * P].bitcast(E5M2),
                    lhsT_scale=sc_deal[:, a * R + t * P : a * R + (t + 1) * P],
                    rhs=u_codes[a][:, chunk[c]].bitcast(E4M3),
                    rhs_scale=u_scales[a][:, chunk[c]],
                    start=(a == 0 and t == 0),
                    stop=(a == PASSES - 1 and t == PACK - 1),
                )

        def deal(copy, dealt, raw):
            copy(dealt.rearrange("p (t m) -> p m t", t=PACK), raw.rearrange("p (m t) -> p m t", t=PACK))

        every = slice(0, J)
        low, high = slice(0, PAIR), slice(PAIR, PACK)
        for ts in (low, high):
            for t in range(ts.start, ts.stop):
                pick(t)
            keep_larger(0, ts, every)
        deal(nc.vector.tensor_copy, w_deal[0][:], w_raw[0][:])
        scale_u(0, every)
        nc.vector.tensor_copy(
            sc_deal[:, 0:wb_at].rearrange("p (a t m) -> p a m t", t=PACK, m=P),
            sc_raw[:, 0:wb_at].rearrange("p (a m t) -> p a m t", t=PACK, m=P),
        )
        quantise(u_codes[0], u_scales[0], u_bf[0], every)
        for t in range(PAIR):
            pick(PACK + t)
        deal(nc.vector.tensor_copy, sc_deal[:, wb_at:], sc_raw[:, wb_at:])
        keep_larger(1, low, every)
        for c in range(CHUNKS):
            first_product(0, c)

        shared = sb.tile([P, PACK * J], F32, name="shared")
        a_first = sb.tile([P, PACK, CH], F32, name="a_first")
        a_abs = [a_first[:], shared[:, 0 : PACK * CH].rearrange("p (t j) -> p t j", t=PACK)]
        a_last = shared[:, PAIR * J : PAIR * J + PACK * CH].rearrange("p (t j) -> p t j", t=PACK)
        peaks = sb.tile([P, CHUNKS, PACK], F32, name="peaks")
        peak = sb.tile([P, PACK], F32, name="peak")
        inv = sb.tile([P, PACK], F32, name="inv")
        factor = sb.tile([P, PACK], F32, name="factor")
        tz_pick = shared[:].rearrange("p (t j) -> p t j", t=PACK)

        deal(nc.vector.tensor_copy, w_deal[1][:], w_raw[1][:])
        for c in range(CHUNKS):
            entries = slice(c * CH // ENTRIES, (c + 1) * CH // ENTRIES)
            for t in range(PAIR):
                gather_on_scalar(first[1][:, PAIR + t, chunk[c]], x_late[:, t, :], list1[:, entries])
                gather_on_scalar(second[1][:, PAIR + t, chunk[c]], x_late[:, t, :], list2[:, entries])
            keep_larger(1, high, chunk[c])
            scale_u(1, chunk[c])
            quantise(u_codes[1], u_scales[1], u_bf[1], chunk[c])
            first_product(1, c)
        deal(nc.scalar.copy, wb_deal[:], wb_raw[:])

        for c in range(CHUNKS - 1):
            nc.scalar.activation(a_abs[c], a_ps[c][:], ABS)
            nc.vector.tensor_reduce(peaks[:, c, :], a_abs[c], AX.X, ALU.max)
        for ts in (low, high):
            nc.scalar.activation(a_last[:, ts, :], a_ps[CHUNKS - 1][:, ts, :], ABS)
            nc.vector.tensor_reduce(peaks[:, CHUNKS - 1, ts], a_last[:, ts, :], AX.X, ALU.max)
        nc.vector.tensor_reduce(peak[:], peaks[:].rearrange("p c t -> p t c"), AX.X, ALU.max)
        nc.vector.reciprocal(inv[:], peak[:])
        nc.vector.tensor_tensor(factor[:], inv[:], us_sb[:], ALU.mult)

        for t in range(PACK):
            gather_on_scalar(tz_pick[:, t, :], tz_sb[t][:], list3[:])

        h_bf = sb.tile([P, J, PACK], BF16, name="h_bf", align_bytes=64)
        h_codes = sb.tile([P, J], U32, name="h_codes", align_bytes=64)
        h_scales = sb.tile([P, J], U8, name="h_scales", align_bytes=64)
        y_sb = [sb.tile([P, PACK, CH], F32, name=f"y{c}") for c in range(CHUNKS)]
        y_bf = sb.tile([P, J, PACK], BF16, name="y_bf", align_bytes=64)
        y_codes = sb.tile([P, J], U32, name="y_codes", align_bytes=64)
        y_scales = sb.tile([P, J], U8, name="y_scales", align_bytes=64)
        out_rows = out_0.rearrange("(p t) j -> p t j", t=PACK)
        out_words = out_1[0].rearrange("p j t -> p (j t)").bitcast(I32)
        wb_bytes = wb_deal[:].bitcast(U8)

        def scale_h(c):
            nc.vector.tensor_tensor(
                h_bf[:, chunk[c], :],
                a_ps[c][:].rearrange("p t j -> p j t"),
                factor[:].unsqueeze(1).to_broadcast([P, CH, PACK]),
                ALU.mult,
            )

        def second_product(c):
            for t in range(PACK):
                nc.tensor.matmul_mx(
                    out=p_ps[c][:, t, :],
                    lhsT=wb_bytes[:, 2 * t * P : 2 * (t + 1) * P].bitcast(E2M1),
                    lhsT_scale=sc_deal[:, wb_at + t * P : wb_at + (t + 1) * P],
                    rhs=h_codes[:, chunk[c]].bitcast(E4M3),
                    rhs_scale=h_scales[:, chunk[c]],
                    start=True,
                    stop=True,
                )

        scale_h(0)
        for c in range(CHUNKS):
            if c + 1 < CHUNKS:
                scale_h(c + 1)
            quantise(h_codes, h_scales, h_bf, chunk[c])
            second_product(c)

        def round_y(copy, c, j0, j1):
            copy(
                y_bf[:, c * CH + j0 : c * CH + j1, :].rearrange("p (c i) t -> p c t i", i=LINE),
                y_sb[c][:, :, j0:j1].rearrange("p t (c i) -> p c t i", i=LINE),
            )

        def store_words(cols):
            quantise(y_codes, y_scales, y_bf, cols)
            nc.sync.dma_start(out=out_words[:, cols], in_=y_codes[:, cols].bitcast(I32))

        for c in range(CHUNKS):
            nc.vector.tensor_tensor(y_sb[c][:], p_ps[c][:], tz_pick[:, :, chunk[c]], ALU.mult)
            nc.sync.dma_start(out=out_rows[:, :, chunk[c]], in_=y_sb[c][:])
            round_y(nc.scalar.copy, c, 0, CH if c + 1 < CHUNKS else CH // 2)
        store_words(slice(0, J - CH))
        round_y(nc.vector.tensor_copy, CHUNKS - 1, CH // 2, CH)
        store_words(chunk[CHUNKS - 1])
        for q in range(QUADS):
            queue = nc.sync if q % 2 == 0 else nc.scalar
            queue.dma_start(out=out_2.bitcast(I32)[0, blocks(q), :], in_=y_scales[live(q), :].bitcast(I32))
